import numpy as np
import ml_dtypes


def mxq(x, axis, fmt="e4m3"):
    dtype, down = {"e4m3": (ml_dtypes.float8_e4m3fn, 7), "e5m2": (ml_dtypes.float8_e5m2, 14)}[fmt]
    v = np.moveaxis(np.asarray(x, np.float32).astype(ml_dtypes.bfloat16).astype(np.float64), axis, -1)
    blocks = v.reshape(v.shape[:-1] + (-1, 32))
    amax = np.abs(blocks).max(-1, keepdims=True)
    byte = np.maximum(np.where(amax > 0, np.frexp(amax)[1] - 1 + 127, 0) - down, 1)
    scale = np.exp2(byte - 127.0)
    codes = (blocks / scale).astype(np.float32).astype(dtype).astype(np.float64)
    return np.moveaxis((codes * scale).reshape(v.shape), -1, axis)


WIDE = False


def mx_kscale(k):
    if not WIDE:
        return np.ones(k)
    levels = np.array([10, -10, 5, -5, 0])
    if k % 512:
        return np.exp2(np.random.permutation(np.resize(levels, k // 32))).repeat(32)
    a = np.empty((k // 512, 16))
    for p in range(k // 512):
        a[p, :8] = np.random.permutation(np.resize(levels, 8))
        for g in range(8):
            far = levels[np.abs(levels - a[p, g]) >= 10]
            a[p, g + 8] = far[np.random.randint(len(far))]
    return np.exp2(a.ravel()).repeat(32)


def f64(x):
    return np.asarray(x).astype(np.float64)


def striped(idx):
    return np.tile(idx.reshape(-1, 16).T, (8, 1)).astype(np.uint16)


def unstriped(offs):
    return offs[:16].T.reshape(-1).astype(np.int64)


def striped8(idx):
    return np.concatenate([x.reshape(-1, 16).T for x in idx]).astype(np.uint16)


def runs(offs, k):
    lists = np.stack([offs[16 * r : 16 * r + 16].T.reshape(-1) for r in range(8)]).astype(np.int64)
    return lists[np.arange(k) % 512 // 64]


def pack_weight(w):
    k, n = w.shape
    w = f64(np.asarray(w, np.float32).astype(ml_dtypes.bfloat16)).reshape(k // 32, 32, n)
    amax = np.abs(w).max(1)
    byte = np.clip(np.where(amax > 0, np.frexp(amax)[1] - 1 + 127 - 7, 1), 1, 254)
    scaled = (w * np.exp2(127.0 - byte)[:, None, :]).reshape(k, n).astype(np.float32)
    words = np.ascontiguousarray(scaled.reshape(k // 512, 128, 4, n).transpose(0, 1, 3, 2)).astype(ml_dtypes.float8_e4m3fn).view(np.uint8)
    return words, np.ascontiguousarray(byte.astype(np.uint8).reshape(k // 512, 16, n))


def unpack_weight(words, scales):
    g, p, n, _ = words.shape
    vals = np.ascontiguousarray(words).view(ml_dtypes.float8_e4m3fn).astype(np.float64) * np.repeat(np.exp2(scales.astype(np.float64) - 127.0), 8, axis=1)[..., None]
    return vals.transpose(0, 1, 3, 2).reshape(g * 512, n)


def relu(v):
    return np.maximum(v, 0.0)


K, T, S, N, G, H = 512, 1024, 512, 512, 2048, 512


def setup_inputs():
    n = np.random.standard_normal
    s = mx_kscale(K)[:, None]
    u = mx_kscale(S)
    packed_xT = pack_weight(n((K, T)) * s)
    packed_dT = pack_weight(n((K, G)) / s)
    return {
        "x_words": packed_xT[0],
        "x_scales": packed_xT[1],
        "d_words": packed_dT[0],
        "d_scales": packed_dT[1],
        "gn": (np.random.uniform(0.5, 1.5, (H, 1)) * u[:, None]).astype(np.float32),
        "w1": (n((H, N)) / np.sqrt(H) / u[:, None]).astype(np.float32),
        "offs": striped(np.random.permutation(T)[:S]),
        "k1": striped8(np.random.randint(0, G, (8, H))),
        "two": striped(np.random.permutation(T)[:S]),
        "k2": striped8(np.random.randint(0, G, (8, H))),
        "n1": striped(np.random.permutation(S)),
        "n2": striped(np.random.permutation(S)),
        "n3": striped(np.random.permutation(S)),
        "n4": striped8(np.stack([np.random.permutation(S) for _ in range(8)])),
        "n5": striped8(np.stack([np.random.permutation(S) for _ in range(8)])),
    }


def reference(x_words, x_scales, d_words, d_scales, gn, w1, offs, k1, two, k2, n1, n2, n3, n4, n5):
    d_k1 = unpack_weight(d_words, d_scales)[np.arange(K)[:, None], runs(k1, K)]
    xq = unpack_weight(x_words, x_scales)[:, unstriped(offs)]
    a = 0.0625 * (d_k1.T @ xq)
    d_k2 = unpack_weight(d_words, d_scales)[np.arange(K)[:, None], runs(k2, K)]
    x_two = unpack_weight(x_words, x_scales)[:, unstriped(two)]
    b = 0.0625 * (d_k2.T @ x_two)
    z = f64(gn) * (np.maximum(np.minimum(a - (0.5 * a[:, unstriped(n1)]), b[:, unstriped(n2)]), b[:, unstriped(n3)]))
    h = mxq(f64(w1), 0, "e4m3").T @ mxq(z, 0, "e4m3")
    pa = h - (h[np.arange(N)[:, None], runs(n4, N)])
    pb = h[np.arange(N)[:, None], runs(n5, N)] - h
    return relu(np.minimum(pa, pb)) - (relu(-1.0 * np.maximum(pa, pb)))

@@ -1,0 +1,267 @@
+from contextlib import ExitStack
+
+import concourse.mybir as mybir
+
+F32 = mybir.dt.float32
+BF16 = mybir.dt.bfloat16
+I32 = mybir.dt.int32
+U32 = mybir.dt.uint32
+U16 = mybir.dt.uint16
+U8 = mybir.dt.uint8
+FP8X4 = mybir.dt.float8_e4m3fn_x4
+ALU = mybir.AluOpType
+ACT = mybir.ActivationFunctionType
+COPY = mybir.ActivationFunctionType.Copy
+
+P = 128
+PACK = 4
+T = 1024
+G = 2048
+S = 512
+HALF = S // 2
+CHUNKS = ((0, 384), (384, 512))
+FLOPS = 3 * 2 * 512 * 512 * 512
+
+
+def tile_picked_twpqclampbminmod_none_p_kernel(
+    tc, x_words, x_scales, d_words, d_scales, gn, w1, offs, k1, two, k2, n1, n2, n3, n4, n5, out
+):
+    nc = tc.nc
+    with ExitStack() as ctx:
+        keep = ctx.enter_context(tc.tile_pool(name="keep", bufs=1))
+        shared = ctx.enter_context(tc.tile_pool(name="shared", bufs=1))
+        psum = ctx.enter_context(tc.psum_pool(name="psum", bufs=1))
+
+        def sb(name, shape, dtype):
+            return keep.tile(shape, dtype, name=name, align_bytes=64)
+
+        def load_list(name, source):
+            tile = sb(name, [P, S // 16], U16)
+            nc.sync.dma_start(tile[:], source)
+            return tile
+
+        def part(offsets, half):
+            return offsets[:, half * HALF // 16 : (half + 1) * HALF // 16]
+
+        def cols(half):
+            return slice(half * HALF, (half + 1) * HALF)
+
+        gain = sb("gain", [P, PACK], F32)
+        nc.sync.dma_start(gain[:], gn.rearrange("(p t) o -> p (t o)", t=PACK))
+        k2_l = load_list("k2_l", k2)
+        d_bytes = sb("d_bytes", [P, G], U8)
+        nc.sync.dma_start(d_bytes[:].bitcast(I32), d_scales[0].bitcast(I32).unsqueeze(1).to_broadcast([16, 8, G // 4]))
+        k1_l = load_list("k1_l", k1)
+        two_l = load_list("two_l", two)
+        offs_l = load_list("offs_l", offs)
+        n2_l = load_list("n2_l", n2)
+        w_raw = [sb("w_raw%d" % half, [P, PACK, HALF], F32) for half in range(2)]
+        w_rows = w1.rearrange("(p j) n -> p j n", j=PACK)
+        x_table = sb("x_table", [P, T], U32)
+        nc.sync.dma_start(x_table[:].bitcast(I32), x_words[0].rearrange("p n r -> p (n r)").bitcast(I32))
+        nc.sync.dma_start(w_raw[0][:], w_rows[:, :, cols(0)])
+        x_bytes = sb("x_bytes", [P, T], U8)
+        d_table = sb("d_table", [P, G], U32)
+        for q in range(4):
+            nc.sync.dma_start(
+                x_bytes[32 * q : 32 * q + 32, :].bitcast(I32),
+                x_scales[0, 4 * q : 4 * q + 4, :].bitcast(I32).unsqueeze(0).to_broadcast([8, 4, T // 4]),
+            )
+        n3_l = load_list("n3_l", n3)
+        nc.sync.dma_start(d_table[:].bitcast(I32), d_words[0].rearrange("p n r -> p (n r)").bitcast(I32))
+        nc.sync.dma_start(w_raw[1][:], w_rows[:, :, cols(1)])
+        n1_l = load_list("n1_l", n1)
+        n4_l = load_list("n4_l", n4)
+        n5_l = load_list("n5_l", n5)
+
+        sign0 = sb("sign0", [P, PACK], F32)
+        nc.scalar.activation(sign0[:], gain[:], ACT.Sign)
+        sign = sb("sign", [P, PACK], F32)
+        nc.scalar.activation(sign[:], sign0[:], ACT.Sign, scale=2.0, bias=1.0)
+        size16 = sb("size16", [P, PACK], F32)
+        nc.scalar.activation(size16[:], gain[:], ACT.Abs, scale=0.0625)
+
+        d_scale = sb("d_scale", [P, 2 * S], U8)
+        nc.gpsimd.memset(d_scale[:].bitcast(I32), 0)
+        picked_bytes = sb("picked_bytes", [P, 2 * S], U8)
+        nc.vector.tensor_copy(picked_bytes[:, 0:S], d_bytes[:].indirect(k2_l[:]))
+        nc.vector.tensor_copy(picked_bytes[:, S : 2 * S], d_bytes[:].indirect(k1_l[:]))
+        dealt_bytes = sb("dealt_bytes", [P, 2 * S], U8)
+        nc.vector.tensor_copy(
+            dealt_bytes[:].rearrange("p (s t m) -> p s t m", s=2, t=PACK),
+            picked_bytes[:].rearrange("p (s m t) -> p s t m", s=2, t=PACK),
+        )
+        for odd in range(2):
+            for e in range(2):
+                nc.sync.dma_start(
+                    d_scale[2 * odd + e : P : 32, :].bitcast(I32), dealt_bytes[16 * odd + 8 * e : P : 32, :].bitcast(I32)
+                )
+
+        w_grouped = sb("w_grouped", [P, PACK, P, PACK], BF16)
+        for half in range(2):
+            w_signed = sb("w_signed%d" % half, [P, PACK, HALF], BF16)
+            for j in range(PACK):
+                nc.scalar.activation(w_signed[:, j, :], w_raw[half][:, j, :], COPY, scale=sign[:, j : j + 1])
+            nc.scalar.copy(
+                w_grouped[:, :, half * P // 2 : (half + 1) * P // 2, :],
+                w_signed[:].rearrange("p j (m t) -> p t m j", t=PACK),
+            )
+
+        def coded_product(name, tokens, codes, scale_col, banks, x_codes, x_scale, picked):
+            nc.vector.tensor_copy(x_codes[:], x_table[:].indirect(tokens[:]))
+            nc.vector.tensor_copy(x_scale[:], x_bytes[:].indirect(tokens[:]))
+            nc.vector.tensor_copy(picked[:], d_table[:].indirect(codes[:]))
+            dealt = sb(name + "_dealt", [P, S], U32)
+            nc.vector.tensor_copy(
+                dealt[:].rearrange("p (t c i) -> p c t i", t=PACK, i=4),
+                picked[:].rearrange("p (c i t) -> p c t i", t=PACK, i=4),
+            )
+            for t in range(PACK):
+                nc.tensor.matmul_mx(
+                    out=banks[t][:],
+                    lhsT=dealt[:, t * P : (t + 1) * P].bitcast(FP8X4),
+                    lhsT_scale=d_scale[:, scale_col + t * P : scale_col + (t + 1) * P],
+                    rhs=x_codes[:].bitcast(FP8X4),
+                    rhs_scale=x_scale[:],
+                    start=True,
+                    stop=True,
+                )
+
+        b_banks = [psum.tile([P, S], F32, name="b_bank%d" % t, tag="bank%d" % t) for t in range(PACK)]
+        b_picked = shared.tile([P, S], U32, name="b_picked", align_bytes=64, offset=1024)
+        coded_product("b", two_l, k2_l, 0, b_banks, sb("b_x_codes", [P, S], U32), sb("b_x_scale", [P, S], U8), b_picked)
+        a_banks = [psum.tile([P, S], F32, name="a_bank%d" % t, tag="bank%d" % (PACK + t)) for t in range(PACK)]
+        a_x_codes = shared.tile([P, S], U32, name="a_x_codes", align_bytes=64, offset=0)
+        a_x_scale = shared.tile([P, S], U8, name="a_x_scale", align_bytes=64, offset=2048)
+        a_picked = shared.tile([P, S], U32, name="a_picked", align_bytes=64, offset=2560)
+        coded_product("a", offs_l, k1_l, S, a_banks, a_x_codes, a_x_scale, a_picked)
+
+        w_codes = shared.tile([P, S], U32, name="w_codes", align_bytes=64, offset=2560)
+        w_scale = sb("w_scale", [P, S], U8)
+        nc.vector.quantize_mx(out=w_codes[:].bitcast(FP8X4), scales=w_scale[:], in_=w_grouped[:].rearrange("p t m j -> p (t m j)"))
+
+        def entries(offsets, lo, hi):
+            return offsets[:, lo // 16 : hi // 16]
+
+        widths = [hi - lo for lo, hi in CHUNKS]
+        b_rows = [sb("b_rows%d" % t, [P, S], F32) for t in range(PACK)]
+        a_rows = [sb("a_rows%d" % t, [P, S], F32) for t in range(PACK)]
+        a_half = [sb("a_half%d" % t, [P, S], F32) for t in range(PACK)]
+        b_n2 = [sb("b_n2_%d" % c, [P, PACK, widths[c]], F32) for c in range(2)]
+        b_n3 = [sb("b_n3_%d" % c, [P, PACK, widths[c]], F32) for c in range(2)]
+        diff = [sb("diff_%d" % c, [P, PACK, widths[c]], F32) for c in range(2)]
+        h_rows = [sb("h_rows%d" % t, [P, S], F32) for t in range(PACK)]
+        h_neg = sb("h_neg", [P, S], F32)
+
+        def empty_b(t):
+            nc.scalar.activation(b_rows[t][:], b_banks[t][:], COPY, scale=size16[:, t : t + 1])
+
+        def empty_a(t):
+            nc.scalar.activation(a_rows[t][:], a_banks[t][:], COPY, scale=size16[:, t : t + 1])
+            nc.vector.tensor_scalar(a_half[t][:], a_rows[t][:], -0.5, None, ALU.mult)
+
+        def fetch_b(target, places, t, c):
+            nc.scalar.activation(target[c][:, t, :], b_rows[t][:].indirect(entries(places, *CHUNKS[c])), COPY)
+
+        def a_less_half(t, c):
+            lo, hi = CHUNKS[c]
+            nc.vector.tensor_tensor(diff[c][:, t, :], a_half[t][:].indirect(entries(n1_l, lo, hi)), a_rows[t][:, lo:hi], ALU.add)
+
+        def quantised_z(c, low, z_grouped):
+            nc.vector.tensor_tensor(low[:], diff[c][:], b_n2[c][:], ALU.min)
+            nc.vector.tensor_tensor(
+                z_grouped[:].rearrange("p (c i) t -> p c t i", i=4),
+                low[:].rearrange("p t (c i) -> p c t i", i=4),
+                b_n3[c][:].rearrange("p t (c i) -> p c t i", i=4),
+                ALU.max,
+            )
+            z_codes = sb("z_codes%d" % c, [P, widths[c]], U32)
+            z_scale = sb("z_scale%d" % c, [P, widths[c]], U8)
+            nc.vector.quantize_mx(out=z_codes[:].bitcast(FP8X4), scales=z_scale[:], in_=z_grouped[:].rearrange("p c t -> p (c t)"))
+            return z_codes, z_scale
+
+        def h_product(target, t, z_codes, z_scale):
+            nc.tensor.matmul_mx(
+                out=target,
+                lhsT=w_codes[:, t * P : (t + 1) * P].bitcast(FP8X4),
+                lhsT_scale=w_scale[:, t * P : (t + 1) * P],
+                rhs=z_codes.bitcast(FP8X4),
+                rhs_scale=z_scale,
+                start=True,
+                stop=True,
+            )
+
+        def empty_h(t, c, source):
+            lo, hi = CHUNKS[c]
+            nc.scalar.copy(h_rows[t][:, lo:hi], source)
+            if t == 0:
+                nc.scalar.activation(h_neg[:, lo:hi], source, COPY, scale=-1.0)
+
+        for t in range(PACK - 1):
+            empty_b(t)
+            fetch_b(b_n2, n2_l, t, 0)
+        empty_a(0)
+        a_less_half(0, 0)
+        empty_b(PACK - 1)
+        fetch_b(b_n2, n2_l, PACK - 1, 0)
+        for t in range(1, PACK):
+            empty_a(t)
+            a_less_half(t, 0)
+            fetch_b(b_n3, n3_l, t - 1, 0)
+        fetch_b(b_n3, n3_l, PACK - 1, 0)
+
+        z_grouped0 = shared.tile([P, widths[0], PACK], BF16, name="z_grouped0", align_bytes=64, offset=8192)
+        z_codes, z_scale = quantised_z(0, sb("low0", [P, PACK, widths[0]], F32), z_grouped0)
+        wide_banks = [psum.tile([P, widths[0]], F32, name="h_bank%d" % t, tag="bank%d" % t) for t in range(PACK)]
+        for t in range(PACK):
+            for lo, hi in ((0, HALF), (HALF, widths[0])):
+                h_product(wide_banks[t][:, lo:hi], t, z_codes[:, lo:hi], z_scale[:, lo:hi])
+
+        for t in range(PACK):
+            fetch_b(b_n2, n2_l, t, 1)
+            a_less_half(t, 1)
+        for t in range(PACK):
+            fetch_b(b_n3, n3_l, t, 1)
+        low1 = shared.tile([P, PACK, widths[1]], F32, name="low1", align_bytes=64, offset=8192)
+        z_codes, z_scale = quantised_z(1, low1, sb("z_grouped1", [P, widths[1], PACK], BF16))
+        last_bank = psum.tile([P, PACK, widths[1]], F32, name="h_bank_last", tag="bank%d" % PACK)
+        for t in range(PACK):
+            h_product(last_bank[:, t, :], t, z_codes[:], z_scale[:])
+
+        for t in range(PACK - 1):
+            empty_h(t, 0, wide_banks[t][:])
+        empty_h(0, 1, last_bank[:, 0, :])
+
+        out_rows = out.rearrange("(p t) n -> p t n", t=PACK)
+        h_n4 = [sb("h_n4_%d" % t, [P, S], F32) for t in range(PACK)]
+        h_n5 = [sb("h_n5_%d" % t, [P, S], F32) for t in range(PACK)]
+
+        def fetch_h(target, places, t, half):
+            nc.scalar.activation(target[t][:, cols(half)], h_rows[t][:].indirect(part(places, half)), COPY)
+
+        def minmod(t, lo, hi, pb):
+            name = "%d_%d" % (t, lo)
+            pa = sb("pa" + name, [P, hi - lo], F32)
+            nc.vector.tensor_tensor(pa[:], h_rows[t][:, lo:hi], h_n4[t][:, lo:hi], ALU.subtract)
+            upper = sb("upper" + name, [P, hi - lo], F32)
+            nc.vector.scalar_tensor_tensor(upper[:], pb, 0.0, pa[:], ALU.max, ALU.min)
+            result = sb("result" + name, [P, hi - lo], F32)
+            nc.vector.scalar_tensor_tensor(result[:], pb, 0.0, upper[:], ALU.min, ALU.max)
+            nc.sync.dma_start(out_rows[:, t, lo:hi], result[:])
+
+        for half in range(2):
+            nc.vector.tensor_tensor(h_n5[0][:, cols(half)], h_rows[0][:].indirect(part(n5_l, half)), h_neg[:, cols(half)], ALU.add)
+            fetch_h(h_n4, n4_l, 0, half)
+        minmod(0, 0, S, h_n5[0][:])
+        empty_h(PACK - 1, 0, wide_banks[PACK - 1][:])
+        for t in range(1, PACK):
+            empty_h(t, 1, last_bank[:, t, :])
+        for t in range(1, PACK):
+            for half in range(2):
+                fetch_h(h_n4, n4_l, t, half)
+                fetch_h(h_n5, n5_l, t, half)
+            pieces = ((0, HALF), (HALF, S)) if t == PACK - 1 else ((0, S),)
+            for lo, hi in pieces:
+                pb = sb("pb%d_%d" % (t, lo), [P, hi - lo], F32)
+                nc.vector.tensor_tensor(pb[:], h_n5[t][:, lo:hi], h_rows[t][:, lo:hi], ALU.subtract)
+                minmod(t, lo, hi, pb[:])

@@ -19,6 +19,7 @@ T = 1024
 G = 2048
 S = 512
 HALF = S // 2
+SPARE = 8
 CHUNKS = ((0, 384), (384, 512))
 FLOPS = 3 * 2 * 512 * 512 * 512
 
@@ -46,20 +47,20 @@ def tile_picked_twpqclampbminmod_none_p_kernel(
         def cols(half):
             return slice(half * HALF, (half + 1) * HALF)
 
-        gain = sb("gain", [P, PACK], F32)
-        nc.sync.dma_start(gain[:], gn.rearrange("(p t) o -> p (t o)", t=PACK))
-        k2_l = load_list("k2_l", k2)
         d_bytes = sb("d_bytes", [P, G], U8)
         nc.sync.dma_start(d_bytes[:].bitcast(I32), d_scales[0].bitcast(I32).unsqueeze(1).to_broadcast([16, 8, G // 4]))
+        k2_l = load_list("k2_l", k2)
+        gain = sb("gain", [P, PACK], F32)
+        nc.sync.dma_start(gain[:], gn.rearrange("(p t) o -> p (t o)", t=PACK))
         k1_l = load_list("k1_l", k1)
         two_l = load_list("two_l", two)
         offs_l = load_list("offs_l", offs)
         n2_l = load_list("n2_l", n2)
-        w_raw = [sb("w_raw%d" % half, [P, PACK, HALF], F32) for half in range(2)]
+        w_early = sb("w_early", [P, PACK, CHUNKS[0][1]], F32)
         w_rows = w1.rearrange("(p j) n -> p j n", j=PACK)
         x_table = sb("x_table", [P, T], U32)
         nc.sync.dma_start(x_table[:].bitcast(I32), x_words[0].rearrange("p n r -> p (n r)").bitcast(I32))
-        nc.sync.dma_start(w_raw[0][:], w_rows[:, :, cols(0)])
+        nc.sync.dma_start(w_early[:], w_rows[:, :, 0 : CHUNKS[0][1]])
         x_bytes = sb("x_bytes", [P, T], U8)
         d_table = sb("d_table", [P, G], U32)
         for q in range(4):
@@ -68,9 +69,10 @@ def tile_picked_twpqclampbminmod_none_p_kernel(
                 x_scales[0, 4 * q : 4 * q + 4, :].bitcast(I32).unsqueeze(0).to_broadcast([8, 4, T // 4]),
             )
         n3_l = load_list("n3_l", n3)
-        nc.sync.dma_start(d_table[:].bitcast(I32), d_words[0].rearrange("p n r -> p (n r)").bitcast(I32))
-        nc.sync.dma_start(w_raw[1][:], w_rows[:, :, cols(1)])
         n1_l = load_list("n1_l", n1)
+        nc.sync.dma_start(d_table[:].bitcast(I32), d_words[0].rearrange("p n r -> p (n r)").bitcast(I32))
+        w_late = sb("w_late", [P, PACK, S - CHUNKS[0][1]], F32)
+        nc.sync.dma_start(w_late[:], w_rows[:, :, CHUNKS[0][1] : S])
         n4_l = load_list("n4_l", n4)
         n5_l = load_list("n5_l", n5)
 
@@ -80,6 +82,9 @@ def tile_picked_twpqclampbminmod_none_p_kernel(
         nc.scalar.activation(sign[:], sign0[:], ACT.Sign, scale=2.0, bias=1.0)
         size16 = sb("size16", [P, PACK], F32)
         nc.scalar.activation(size16[:], gain[:], ACT.Abs, scale=0.0625)
+
+        size_half = sb("size_half", [P, PACK], F32)
+        nc.scalar.activation(size_half[:], size16[:], COPY, scale=-0.5)
 
         d_scale = sb("d_scale", [P, 2 * S], U8)
         nc.gpsimd.memset(d_scale[:].bitcast(I32), 0)
@@ -98,24 +103,24 @@ def tile_picked_twpqclampbminmod_none_p_kernel(
                 )
 
         w_grouped = sb("w_grouped", [P, PACK, P, PACK], BF16)
-        for half in range(2):
-            w_signed = sb("w_signed%d" % half, [P, PACK, HALF], BF16)
+        for (lo, hi), w_raw in zip(CHUNKS, (w_early, w_late)):
+            w_signed = sb("w_signed%d" % lo, [P, PACK, hi - lo], BF16)
             for j in range(PACK):
-                nc.scalar.activation(w_signed[:, j, :], w_raw[half][:, j, :], COPY, scale=sign[:, j : j + 1])
+                nc.scalar.activation(w_signed[:, j, :], w_raw[:, j, :], COPY, scale=sign[:, j : j + 1])
             nc.scalar.copy(
-                w_grouped[:, :, half * P // 2 : (half + 1) * P // 2, :],
-                w_signed[:].rearrange("p j (m t) -> p t m j", t=PACK),
+                w_grouped[:, :, lo // PACK : hi // PACK, :].rearrange("p t (b i) j -> p b j i t", i=2),
+                w_signed[:].rearrange("p j (b i t) -> p b j i t", i=2, t=PACK),
             )
 
         def coded_product(name, tokens, codes, scale_col, banks, x_codes, x_scale, picked):
-            nc.vector.tensor_copy(x_codes[:], x_table[:].indirect(tokens[:]))
-            nc.vector.tensor_copy(x_scale[:], x_bytes[:].indirect(tokens[:]))
             nc.vector.tensor_copy(picked[:], d_table[:].indirect(codes[:]))
+            nc.vector.tensor_copy(x_codes[:], x_table[:].indirect(tokens[:]))
             dealt = sb(name + "_dealt", [P, S], U32)
             nc.vector.tensor_copy(
                 dealt[:].rearrange("p (t c i) -> p c t i", t=PACK, i=4),
                 picked[:].rearrange("p (c i t) -> p c t i", t=PACK, i=4),
             )
+            nc.vector.tensor_copy(x_scale[:], x_bytes[:].indirect(tokens[:]))
             for t in range(PACK):
                 nc.tensor.matmul_mx(
                     out=banks[t][:],
@@ -140,128 +145,122 @@ def tile_picked_twpqclampbminmod_none_p_kernel(
         w_scale = sb("w_scale", [P, S], U8)
         nc.vector.quantize_mx(out=w_codes[:].bitcast(FP8X4), scales=w_scale[:], in_=w_grouped[:].rearrange("p t m j -> p (t m j)"))
 
-        def entries(offsets, lo, hi):
-            return offsets[:, lo // 16 : hi // 16]
+        def window(name):
+            tile = sb(name, [P, S + SPARE], F32)
+            nc.gpsimd.memset(tile[:, S : S + SPARE], 0.0)
+            return tile
 
         widths = [hi - lo for lo, hi in CHUNKS]
-        b_rows = [sb("b_rows%d" % t, [P, S], F32) for t in range(PACK)]
-        a_rows = [sb("a_rows%d" % t, [P, S], F32) for t in range(PACK)]
-        a_half = [sb("a_half%d" % t, [P, S], F32) for t in range(PACK)]
-        b_n2 = [sb("b_n2_%d" % c, [P, PACK, widths[c]], F32) for c in range(2)]
+        last = PACK - 1
+        b_rows = [window("b_rows%d" % t) for t in range(PACK)]
+        a_half = [window("a_half%d" % t) for t in range(PACK)]
+        a_rows = [sb("a_rows%d" % t, [P, S], F32) for t in range(last)]
+        h_wide = [sb("h_wide%d" % t, [P, 2 * S], F32) for t in range(PACK)]
+        neg_wide = sb("neg_wide", [P, 2 * S], F32)
+        h_rows = [tile[:, 0:S] for tile in h_wide]
+        diff = [tile[:, S : 2 * S] for tile in h_wide]
+        h_neg = neg_wide[:, 0:S]
+        b_n2 = [neg_wide[:, S : 2 * S]] + [sb("b_n2_%d" % t, [P, S], F32)[:] for t in range(1, PACK)]
         b_n3 = [sb("b_n3_%d" % c, [P, PACK, widths[c]], F32) for c in range(2)]
-        diff = [sb("diff_%d" % c, [P, PACK, widths[c]], F32) for c in range(2)]
-        h_rows = [sb("h_rows%d" % t, [P, S], F32) for t in range(PACK)]
-        h_neg = sb("h_neg", [P, S], F32)
+        low = sb("low", [P, PACK, S], F32)
 
         def empty_b(t):
-            nc.scalar.activation(b_rows[t][:], b_banks[t][:], COPY, scale=size16[:, t : t + 1])
+            nc.scalar.activation(b_rows[t][:, 0:S], b_banks[t][:], COPY, scale=size16[:, t : t + 1])
+
+        def fetch_n2(t):
+            nc.scalar.activation(b_n2[t], b_rows[t][:].indirect(n2_l[:]), COPY)
 
         def empty_a(t):
             nc.scalar.activation(a_rows[t][:], a_banks[t][:], COPY, scale=size16[:, t : t + 1])
-            nc.vector.tensor_scalar(a_half[t][:], a_rows[t][:], -0.5, None, ALU.mult)
 
-        def fetch_b(target, places, t, c):
-            nc.scalar.activation(target[c][:, t, :], b_rows[t][:].indirect(entries(places, *CHUNKS[c])), COPY)
+        def halve(t):
+            nc.vector.tensor_scalar(a_half[t][:, 0:S], a_rows[t][:], -0.5, None, ALU.mult)
 
-        def a_less_half(t, c):
-            lo, hi = CHUNKS[c]
-            nc.vector.tensor_tensor(diff[c][:, t, :], a_half[t][:].indirect(entries(n1_l, lo, hi)), a_rows[t][:, lo:hi], ALU.add)
+        def a_less_half(t):
+            nc.vector.tensor_tensor(diff[t], a_half[t][:].indirect(n1_l[:]), a_rows[t][:], ALU.add)
 
-        def quantised_z(c, low, z_grouped):
-            nc.vector.tensor_tensor(low[:], diff[c][:], b_n2[c][:], ALU.min)
+        def smaller(t):
+            nc.vector.tensor_tensor(low[:, t, :], diff[t], b_n2[t], ALU.min)
+
+        for t in range(last):
+            empty_b(t)
+            fetch_n2(t)
+        nc.vector.tensor_scalar(b_rows[last][:, 0:S], b_banks[last][:], size16[:, last : last + 1], None, ALU.mult)
+        nc.vector.tensor_scalar(a_half[0][:, 0:S], a_banks[0][:], size_half[:, 0:1], None, ALU.mult)
+        nc.vector.tensor_scalar(a_rows[0][:], a_half[0][:, 0:S], -2.0, None, ALU.mult)
+        a_less_half(0)
+        for t in range(1, last):
+            empty_a(t)
+            halve(t)
+            smaller(t - 1)
+            a_less_half(t)
+        nc.scalar.activation(a_half[last][:, 0:S], a_banks[last][:], COPY, scale=size_half[:, last : last + 1])
+        fetch_n2(last)
+        a_n1 = sb("a_n1", [P, S], F32)
+        nc.scalar.activation(a_n1[:], a_half[last][:].indirect(n1_l[:]), COPY)
+        nc.vector.scalar_tensor_tensor(diff[last], a_banks[last][:], size16[:, last : last + 1], a_n1[:], ALU.mult, ALU.add)
+        smaller(last - 1)
+        smaller(last)
+
+        z_grouped = [sb("z_grouped%d" % c, [P, widths[c], PACK], BF16) for c in range(2)]
+        for c, (lo, hi) in enumerate(CHUNKS):
+            for t in range(PACK):
+                nc.scalar.activation(b_n3[c][:, t, :], b_rows[t][:].indirect(n3_l[:, lo // 16 : hi // 16]), COPY)
             nc.vector.tensor_tensor(
-                z_grouped[:].rearrange("p (c i) t -> p c t i", i=4),
-                low[:].rearrange("p t (c i) -> p c t i", i=4),
+                z_grouped[c][:].rearrange("p (c i) t -> p c t i", i=4),
+                low[:, :, lo:hi].rearrange("p t (c i) -> p c t i", i=4),
                 b_n3[c][:].rearrange("p t (c i) -> p c t i", i=4),
                 ALU.max,
             )
-            z_codes = sb("z_codes%d" % c, [P, widths[c]], U32)
-            z_scale = sb("z_scale%d" % c, [P, widths[c]], U8)
-            nc.vector.quantize_mx(out=z_codes[:].bitcast(FP8X4), scales=z_scale[:], in_=z_grouped[:].rearrange("p c t -> p (c t)"))
-            return z_codes, z_scale
-
-        def h_product(target, t, z_codes, z_scale):
-            nc.tensor.matmul_mx(
-                out=target,
-                lhsT=w_codes[:, t * P : (t + 1) * P].bitcast(FP8X4),
-                lhsT_scale=w_scale[:, t * P : (t + 1) * P],
-                rhs=z_codes.bitcast(FP8X4),
-                rhs_scale=z_scale,
-                start=True,
-                stop=True,
+        z_codes = sb("z_codes", [P, S], U32)
+        z_scale = sb("z_scale", [P, S], U8)
+        for c, (lo, hi) in enumerate(CHUNKS):
+            nc.vector.quantize_mx(
+                out=z_codes[:, lo:hi].bitcast(FP8X4), scales=z_scale[:, lo:hi], in_=z_grouped[c][:].rearrange("p c t -> p (c t)")
             )
-
-        def empty_h(t, c, source):
-            lo, hi = CHUNKS[c]
-            nc.scalar.copy(h_rows[t][:, lo:hi], source)
-            if t == 0:
-                nc.scalar.activation(h_neg[:, lo:hi], source, COPY, scale=-1.0)
-
-        for t in range(PACK - 1):
-            empty_b(t)
-            fetch_b(b_n2, n2_l, t, 0)
-        empty_a(0)
-        a_less_half(0, 0)
-        empty_b(PACK - 1)
-        fetch_b(b_n2, n2_l, PACK - 1, 0)
-        for t in range(1, PACK):
-            empty_a(t)
-            a_less_half(t, 0)
-            fetch_b(b_n3, n3_l, t - 1, 0)
-        fetch_b(b_n3, n3_l, PACK - 1, 0)
-
-        z_grouped0 = shared.tile([P, widths[0], PACK], BF16, name="z_grouped0", align_bytes=64, offset=8192)
-        z_codes, z_scale = quantised_z(0, sb("low0", [P, PACK, widths[0]], F32), z_grouped0)
-        wide_banks = [psum.tile([P, widths[0]], F32, name="h_bank%d" % t, tag="bank%d" % t) for t in range(PACK)]
+        first_banks = [psum.tile([P, HALF], F32, name="h_first%d" % half, tag="bank%d" % (PACK * half)) for half in range(2)]
+        h_banks = {t: psum.tile([P, S], F32, name="h_bank%d" % t, tag="bank%d" % t) for t in range(1, PACK)}
         for t in range(PACK):
-            for lo, hi in ((0, HALF), (HALF, widths[0])):
-                h_product(wide_banks[t][:, lo:hi], t, z_codes[:, lo:hi], z_scale[:, lo:hi])
-
-        for t in range(PACK):
-            fetch_b(b_n2, n2_l, t, 1)
-            a_less_half(t, 1)
-        for t in range(PACK):
-            fetch_b(b_n3, n3_l, t, 1)
-        low1 = shared.tile([P, PACK, widths[1]], F32, name="low1", align_bytes=64, offset=8192)
-        z_codes, z_scale = quantised_z(1, low1, sb("z_grouped1", [P, widths[1], PACK], BF16))
-        last_bank = psum.tile([P, PACK, widths[1]], F32, name="h_bank_last", tag="bank%d" % PACK)
-        for t in range(PACK):
-            h_product(last_bank[:, t, :], t, z_codes[:], z_scale[:])
-
-        for t in range(PACK - 1):
-            empty_h(t, 0, wide_banks[t][:])
-        empty_h(0, 1, last_bank[:, 0, :])
+            for lo, hi in ((0, HALF), (HALF, widths[0]), CHUNKS[1]):
+                nc.tensor.matmul_mx(
+                    out=h_banks[t][:, lo:hi] if t else first_banks[lo // HALF][:, lo % HALF : lo % HALF + hi - lo],
+                    lhsT=w_codes[:, t * P : (t + 1) * P].bitcast(FP8X4),
+                    lhsT_scale=w_scale[:, t * P : (t + 1) * P],
+                    rhs=z_codes[:, lo:hi].bitcast(FP8X4),
+                    rhs_scale=z_scale[:, lo:hi],
+                    start=True,
+                    stop=True,
+                )
 
         out_rows = out.rearrange("(p t) n -> p t n", t=PACK)
-        h_n4 = [sb("h_n4_%d" % t, [P, S], F32) for t in range(PACK)]
-        h_n5 = [sb("h_n5_%d" % t, [P, S], F32) for t in range(PACK)]
+        pa = [sb("pa%d" % t, [P, S], F32) for t in range(PACK)]
+        pb = [sb("pb%d" % t, [P, S], F32) for t in range(PACK)]
+        upper = [sb("upper%d" % t, [P, S], F32) for t in range(PACK)]
+        h_n4 = {t: sb("h_n4_%d" % t, [P, S], F32) for t in range(1, PACK)}
+        h_n5 = {t: sb("h_n5_%d" % t, [P, S], F32) for t in range(1, PACK)}
 
-        def fetch_h(target, places, t, half):
-            nc.scalar.activation(target[t][:, cols(half)], h_rows[t][:].indirect(part(places, half)), COPY)
+        def clamp_above(t, lo, hi):
+            nc.vector.scalar_tensor_tensor(upper[t][:, lo:hi], pb[t][:, lo:hi], 0.0, pa[t][:, lo:hi], ALU.max, ALU.min)
 
-        def minmod(t, lo, hi, pb):
-            name = "%d_%d" % (t, lo)
-            pa = sb("pa" + name, [P, hi - lo], F32)
-            nc.vector.tensor_tensor(pa[:], h_rows[t][:, lo:hi], h_n4[t][:, lo:hi], ALU.subtract)
-            upper = sb("upper" + name, [P, hi - lo], F32)
-            nc.vector.scalar_tensor_tensor(upper[:], pb, 0.0, pa[:], ALU.max, ALU.min)
-            result = sb("result" + name, [P, hi - lo], F32)
-            nc.vector.scalar_tensor_tensor(result[:], pb, 0.0, upper[:], ALU.min, ALU.max)
+        def clamp_below(t, lo, hi):
+            result = sb("result%d_%d" % (t, lo), [P, hi - lo], F32)
+            nc.vector.scalar_tensor_tensor(result[:], pb[t][:, lo:hi], 0.0, upper[t][:, lo:hi], ALU.min, ALU.max)
             nc.sync.dma_start(out_rows[:, t, lo:hi], result[:])
 
         for half in range(2):
-            nc.vector.tensor_tensor(h_n5[0][:, cols(half)], h_rows[0][:].indirect(part(n5_l, half)), h_neg[:, cols(half)], ALU.add)
-            fetch_h(h_n4, n4_l, 0, half)
-        minmod(0, 0, S, h_n5[0][:])
-        empty_h(PACK - 1, 0, wide_banks[PACK - 1][:])
+            nc.scalar.copy(h_wide[0][:, cols(half)], first_banks[half][:])
+            nc.vector.tensor_scalar(neg_wide[:, cols(half)], first_banks[half][:], -1.0, None, ALU.mult)
+        nc.vector.tensor_tensor(pa[0][:], neg_wide[:].indirect(n4_l[:]), h_rows[0], ALU.add)
+        nc.vector.tensor_tensor(pb[0][:], h_wide[0][:].indirect(n5_l[:]), h_neg, ALU.add)
         for t in range(1, PACK):
-            empty_h(t, 1, last_bank[:, t, :])
-        for t in range(1, PACK):
-            for half in range(2):
-                fetch_h(h_n4, n4_l, t, half)
-                fetch_h(h_n5, n5_l, t, half)
-            pieces = ((0, HALF), (HALF, S)) if t == PACK - 1 else ((0, S),)
-            for lo, hi in pieces:
-                pb = sb("pb%d_%d" % (t, lo), [P, hi - lo], F32)
-                nc.vector.tensor_tensor(pb[:], h_n5[t][:, lo:hi], h_rows[t][:, lo:hi], ALU.subtract)
-                minmod(t, lo, hi, pb[:])
+            nc.scalar.copy(h_rows[t], h_banks[t][:])
+            nc.scalar.activation(h_n4[t][:], h_wide[t][:].indirect(n4_l[:]), COPY)
+            nc.scalar.activation(h_n5[t][:], h_wide[t][:].indirect(n5_l[:]), COPY)
+            nc.vector.tensor_tensor(pa[t][:], h_rows[t], h_n4[t][:], ALU.subtract)
+            clamp_above(t - 1, 0, S)
+            nc.vector.tensor_tensor(pb[t][:], h_n5[t][:], h_rows[t], ALU.subtract)
+            clamp_below(t - 1, 0, S)
+        for half in range(2):
+            clamp_above(last, half * HALF, (half + 1) * HALF)
+        for half in range(2):
+            clamp_below(last, half * HALF, (half + 1) * HALF)

@@ -108,8 +108,8 @@ def tile_picked_twpqclampbminmod_none_p_kernel(
             for j in range(PACK):
                 nc.scalar.activation(w_signed[:, j, :], w_raw[:, j, :], COPY, scale=sign[:, j : j + 1])
             nc.scalar.copy(
-                w_grouped[:, :, lo // PACK : hi // PACK, :].rearrange("p t (b i) j -> p b j i t", i=2),
-                w_signed[:].rearrange("p j (b i t) -> p b j i t", i=2, t=PACK),
+                w_grouped[:, :, lo // PACK : hi // PACK, :].rearrange("p t (b i) j -> p b t i j", i=2),
+                w_signed[:].rearrange("p j (b i t) -> p b t i j", i=2, t=PACK),
             )
 
         def coded_product(name, tokens, codes, scale_col, banks, x_codes, x_scale, picked):
@@ -200,16 +200,17 @@ def tile_picked_twpqclampbminmod_none_p_kernel(
         nc.scalar.activation(a_n1[:], a_half[last][:].indirect(n1_l[:]), COPY)
         nc.vector.scalar_tensor_tensor(diff[last], a_banks[last][:], size16[:, last : last + 1], a_n1[:], ALU.mult, ALU.add)
         smaller(last - 1)
-        smaller(last)
+        for lo, hi in CHUNKS:
+            nc.vector.tensor_tensor(low[:, last, lo:hi], h_wide[last][:, S + lo : S + hi], b_n2[last][:, lo:hi], ALU.min)
 
         z_grouped = [sb("z_grouped%d" % c, [P, widths[c], PACK], BF16) for c in range(2)]
         for c, (lo, hi) in enumerate(CHUNKS):
             for t in range(PACK):
                 nc.scalar.activation(b_n3[c][:, t, :], b_rows[t][:].indirect(n3_l[:, lo // 16 : hi // 16]), COPY)
             nc.vector.tensor_tensor(
-                z_grouped[c][:].rearrange("p (c i) t -> p c t i", i=4),
-                low[:, :, lo:hi].rearrange("p t (c i) -> p c t i", i=4),
-                b_n3[c][:].rearrange("p t (c i) -> p c t i", i=4),
+                z_grouped[c][:].rearrange("p (c i) t -> p c t i", i=2),
+                low[:, :, lo:hi].rearrange("p t (c i) -> p c t i", i=2),
+                b_n3[c][:].rearrange("p t (c i) -> p c t i", i=2),
                 ALU.max,
             )
         z_codes = sb("z_codes", [P, S], U32)

@@ -48,10 +48,12 @@ def tile_picked_twpqclampbminmod_none_p_kernel(
             return slice(half * HALF, (half + 1) * HALF)
 
         d_bytes = sb("d_bytes", [P, G], U8)
-        nc.sync.dma_start(d_bytes[:].bitcast(I32), d_scales[0].bitcast(I32).unsqueeze(1).to_broadcast([16, 8, G // 4]))
-        k2_l = load_list("k2_l", k2)
+        nc.vector.memset(d_bytes[:].bitcast(I32), 0)
+        for e in range(2):
+            nc.sync.dma_start(d_bytes[e:P:16, :].bitcast(I32), d_scales[0, e:16:2, :].bitcast(I32))
         gain = sb("gain", [P, PACK], F32)
-        nc.sync.dma_start(gain[:], gn.rearrange("(p t) o -> p (t o)", t=PACK))
+        nc.gpsimd.dma_start(gain[:], gn.rearrange("(p t) o -> p (t o)", t=PACK))
+        k2_l = load_list("k2_l", k2)
         k1_l = load_list("k1_l", k1)
         two_l = load_list("two_l", two)
         offs_l = load_list("offs_l", offs)
@@ -62,14 +64,12 @@ def tile_picked_twpqclampbminmod_none_p_kernel(
         nc.sync.dma_start(x_table[:].bitcast(I32), x_words[0].rearrange("p n r -> p (n r)").bitcast(I32))
         nc.sync.dma_start(w_early[:], w_rows[:, :, 0 : CHUNKS[0][1]])
         x_bytes = sb("x_bytes", [P, T], U8)
-        d_table = sb("d_table", [P, G], U32)
+        nc.vector.memset(x_bytes[:].bitcast(I32), 0)
         for q in range(4):
-            nc.sync.dma_start(
-                x_bytes[32 * q : 32 * q + 32, :].bitcast(I32),
-                x_scales[0, 4 * q : 4 * q + 4, :].bitcast(I32).unsqueeze(0).to_broadcast([8, 4, T // 4]),
-            )
+            nc.sync.dma_start(x_bytes[32 * q : 32 * q + 4, :].bitcast(I32), x_scales[0, 4 * q : 4 * q + 4, :].bitcast(I32))
         n3_l = load_list("n3_l", n3)
         n1_l = load_list("n1_l", n1)
+        d_table = sb("d_table", [P, G], U32)
         nc.sync.dma_start(d_table[:].bitcast(I32), d_words[0].rearrange("p n r -> p (n r)").bitcast(I32))
         w_late = sb("w_late", [P, PACK, S - CHUNKS[0][1]], F32)
         nc.sync.dma_start(w_late[:], w_rows[:, :, CHUNKS[0][1] : S])
@@ -87,7 +87,7 @@ def tile_picked_twpqclampbminmod_none_p_kernel(
         nc.scalar.activation(size_half[:], size16[:], COPY, scale=-0.5)
 
         d_scale = sb("d_scale", [P, 2 * S], U8)
-        nc.gpsimd.memset(d_scale[:].bitcast(I32), 0)
+        nc.vector.memset(d_scale[:].bitcast(I32), 0)
         picked_bytes = sb("picked_bytes", [P, 2 * S], U8)
         nc.vector.tensor_copy(picked_bytes[:, 0:S], d_bytes[:].indirect(k2_l[:]))
         nc.vector.tensor_copy(picked_bytes[:, S : 2 * S], d_bytes[:].indirect(k1_l[:]))
@@ -99,7 +99,7 @@ def tile_picked_twpqclampbminmod_none_p_kernel(
         for odd in range(2):
             for e in range(2):
                 nc.sync.dma_start(
-                    d_scale[2 * odd + e : P : 32, :].bitcast(I32), dealt_bytes[16 * odd + 8 * e : P : 32, :].bitcast(I32)
+                    d_scale[2 * odd + e : P : 32, :].bitcast(I32), dealt_bytes[16 * odd + e : P : 32, :].bitcast(I32)
                 )
 
         w_grouped = sb("w_grouped", [P, PACK, P, PACK], BF16)

from contextlib import ExitStack

import concourse.mybir as mybir

F32 = mybir.dt.float32
BF16 = mybir.dt.bfloat16
I32 = mybir.dt.int32
U32 = mybir.dt.uint32
U16 = mybir.dt.uint16
U8 = mybir.dt.uint8
FP8X4 = mybir.dt.float8_e4m3fn_x4
ALU = mybir.AluOpType
ACT = mybir.ActivationFunctionType
COPY = mybir.ActivationFunctionType.Copy

P = 128
PACK = 4
T = 1024
G = 2048
S = 512
HALF = S // 2
SPARE = 8
CHUNKS = ((0, 384), (384, 512))
FLOPS = 3 * 2 * 512 * 512 * 512


def tile_picked_twpqclampbminmod_none_p_kernel(
    tc, x_words, x_scales, d_words, d_scales, gn, w1, offs, k1, two, k2, n1, n2, n3, n4, n5, out
):
    nc = tc.nc
    with ExitStack() as ctx:
        keep = ctx.enter_context(tc.tile_pool(name="keep", bufs=1))
        shared = ctx.enter_context(tc.tile_pool(name="shared", bufs=1))
        psum = ctx.enter_context(tc.psum_pool(name="psum", bufs=1))

        def sb(name, shape, dtype):
            return keep.tile(shape, dtype, name=name, align_bytes=64)

        def load_list(name, source):
            tile = sb(name, [P, S // 16], U16)
            nc.sync.dma_start(tile[:], source)
            return tile

        def part(offsets, half):
            return offsets[:, half * HALF // 16 : (half + 1) * HALF // 16]

        def cols(half):
            return slice(half * HALF, (half + 1) * HALF)

        d_bytes = sb("d_bytes", [P, G], U8)
        nc.vector.memset(d_bytes[:].bitcast(I32), 0)
        for e in range(2):
            nc.sync.dma_start(d_bytes[e:P:16, :].bitcast(I32), d_scales[0, e:16:2, :].bitcast(I32))
        gain = sb("gain", [P, PACK], F32)
        nc.gpsimd.dma_start(gain[:], gn.rearrange("(p t) o -> p (t o)", t=PACK))
        k2_l = load_list("k2_l", k2)
        k1_l = load_list("k1_l", k1)
        two_l = load_list("two_l", two)
        offs_l = load_list("offs_l", offs)
        n2_l = load_list("n2_l", n2)
        w_early = sb("w_early", [P, PACK, CHUNKS[0][1]], F32)
        w_rows = w1.rearrange("(p j) n -> p j n", j=PACK)
        x_table = sb("x_table", [P, T], U32)
        nc.sync.dma_start(x_table[:].bitcast(I32), x_words[0].rearrange("p n r -> p (n r)").bitcast(I32))
        nc.sync.dma_start(w_early[:], w_rows[:, :, 0 : CHUNKS[0][1]])
        x_bytes = sb("x_bytes", [P, T], U8)
        nc.vector.memset(x_bytes[:].bitcast(I32), 0)
        for q in range(4):
            nc.sync.dma_start(x_bytes[32 * q : 32 * q + 4, :].bitcast(I32), x_scales[0, 4 * q : 4 * q + 4, :].bitcast(I32))
        n3_l = load_list("n3_l", n3)
        n1_l = load_list("n1_l", n1)
        d_table = sb("d_table", [P, G], U32)
        nc.sync.dma_start(d_table[:].bitcast(I32), d_words[0].rearrange("p n r -> p (n r)").bitcast(I32))
        w_late = sb("w_late", [P, PACK, S - CHUNKS[0][1]], F32)
        nc.sync.dma_start(w_late[:], w_rows[:, :, CHUNKS[0][1] : S])
        n4_l = load_list("n4_l", n4)
        n5_l = load_list("n5_l", n5)

        sign0 = sb("sign0", [P, PACK], F32)
        nc.scalar.activation(sign0[:], gain[:], ACT.Sign)
        sign = sb("sign", [P, PACK], F32)
        nc.scalar.activation(sign[:], sign0[:], ACT.Sign, scale=2.0, bias=1.0)
        size16 = sb("size16", [P, PACK], F32)
        nc.scalar.activation(size16[:], gain[:], ACT.Abs, scale=0.0625)

        size_half = sb("size_half", [P, PACK], F32)
        nc.scalar.activation(size_half[:], size16[:], COPY, scale=-0.5)

        d_scale = sb("d_scale", [P, 2 * S], U8)
        nc.vector.memset(d_scale[:].bitcast(I32), 0)
        picked_bytes = sb("picked_bytes", [P, 2 * S], U8)
        nc.vector.tensor_copy(picked_bytes[:, 0:S], d_bytes[:].indirect(k2_l[:]))
        nc.vector.tensor_copy(picked_bytes[:, S : 2 * S], d_bytes[:].indirect(k1_l[:]))
        dealt_bytes = sb("dealt_bytes", [P, 2 * S], U8)
        nc.vector.tensor_copy(
            dealt_bytes[:].rearrange("p (s t m) -> p s t m", s=2, t=PACK),
            picked_bytes[:].rearrange("p (s m t) -> p s t m", s=2, t=PACK),
        )
        for odd in range(2):
            for e in range(2):
                nc.sync.dma_start(
                    d_scale[2 * odd + e : P : 32, :].bitcast(I32), dealt_bytes[16 * odd + e : P : 32, :].bitcast(I32)
                )

        w_grouped = sb("w_grouped", [P, PACK, P, PACK], BF16)
        for (lo, hi), w_raw in zip(CHUNKS, (w_early, w_late)):
            w_signed = sb("w_signed%d" % lo, [P, PACK, hi - lo], BF16)
            for j in range(PACK):
                nc.scalar.activation(w_signed[:, j, :], w_raw[:, j, :], COPY, scale=sign[:, j : j + 1])
            nc.scalar.copy(
                w_grouped[:, :, lo // PACK : hi // PACK, :].rearrange("p t (b i) j -> p b t i j", i=2),
                w_signed[:].rearrange("p j (b i t) -> p b t i j", i=2, t=PACK),
            )

        def coded_product(name, tokens, codes, scale_col, banks, x_codes, x_scale, picked):
            nc.vector.tensor_copy(picked[:], d_table[:].indirect(codes[:]))
            nc.vector.tensor_copy(x_codes[:], x_table[:].indirect(tokens[:]))
            dealt = sb(name + "_dealt", [P, S], U32)
            nc.vector.tensor_copy(
                dealt[:].rearrange("p (t c i) -> p c t i", t=PACK, i=4),
                picked[:].rearrange("p (c i t) -> p c t i", t=PACK, i=4),
            )
            nc.vector.tensor_copy(x_scale[:], x_bytes[:].indirect(tokens[:]))
            for t in range(PACK):
                nc.tensor.matmul_mx(
                    out=banks[t][:],
                    lhsT=dealt[:, t * P : (t + 1) * P].bitcast(FP8X4),
                    lhsT_scale=d_scale[:, scale_col + t * P : scale_col + (t + 1) * P],
                    rhs=x_codes[:].bitcast(FP8X4),
                    rhs_scale=x_scale[:],
                    start=True,
                    stop=True,
                )

        b_banks = [psum.tile([P, S], F32, name="b_bank%d" % t, tag="bank%d" % t) for t in range(PACK)]
        b_picked = shared.tile([P, S], U32, name="b_picked", align_bytes=64, offset=1024)
        coded_product("b", two_l, k2_l, 0, b_banks, sb("b_x_codes", [P, S], U32), sb("b_x_scale", [P, S], U8), b_picked)
        a_banks = [psum.tile([P, S], F32, name="a_bank%d" % t, tag="bank%d" % (PACK + t)) for t in range(PACK)]
        a_x_codes = shared.tile([P, S], U32, name="a_x_codes", align_bytes=64, offset=0)
        a_x_scale = shared.tile([P, S], U8, name="a_x_scale", align_bytes=64, offset=2048)
        a_picked = shared.tile([P, S], U32, name="a_picked", align_bytes=64, offset=2560)
        coded_product("a", offs_l, k1_l, S, a_banks, a_x_codes, a_x_scale, a_picked)

        w_codes = shared.tile([P, S], U32, name="w_codes", align_bytes=64, offset=2560)
        w_scale = sb("w_scale", [P, S], U8)
        nc.vector.quantize_mx(out=w_codes[:].bitcast(FP8X4), scales=w_scale[:], in_=w_grouped[:].rearrange("p t m j -> p (t m j)"))

        def window(name):
            tile = sb(name, [P, S + SPARE], F32)
            nc.gpsimd.memset(tile[:, S : S + SPARE], 0.0)
            return tile

        widths = [hi - lo for lo, hi in CHUNKS]
        last = PACK - 1
        b_rows = [window("b_rows%d" % t) for t in range(PACK)]
        a_half = [window("a_half%d" % t) for t in range(PACK)]
        a_rows = [sb("a_rows%d" % t, [P, S], F32) for t in range(last)]
        h_wide = [sb("h_wide%d" % t, [P, 2 * S], F32) for t in range(PACK)]
        neg_wide = sb("neg_wide", [P, 2 * S], F32)
        h_rows = [tile[:, 0:S] for tile in h_wide]
        diff = [tile[:, S : 2 * S] for tile in h_wide]
        h_neg = neg_wide[:, 0:S]
        b_n2 = [neg_wide[:, S : 2 * S]] + [sb("b_n2_%d" % t, [P, S], F32)[:] for t in range(1, PACK)]
        b_n3 = [sb("b_n3_%d" % c, [P, PACK, widths[c]], F32) for c in range(2)]
        low = sb("low", [P, PACK, S], F32)

        def empty_b(t):
            nc.scalar.activation(b_rows[t][:, 0:S], b_banks[t][:], COPY, scale=size16[:, t : t + 1])

        def fetch_n2(t):
            nc.scalar.activation(b_n2[t], b_rows[t][:].indirect(n2_l[:]), COPY)

        def empty_a(t):
            nc.scalar.activation(a_rows[t][:], a_banks[t][:], COPY, scale=size16[:, t : t + 1])

        def halve(t):
            nc.vector.tensor_scalar(a_half[t][:, 0:S], a_rows[t][:], -0.5, None, ALU.mult)

        def a_less_half(t):
            nc.vector.tensor_tensor(diff[t], a_half[t][:].indirect(n1_l[:]), a_rows[t][:], ALU.add)

        def smaller(t):
            nc.vector.tensor_tensor(low[:, t, :], diff[t], b_n2[t], ALU.min)

        for t in range(last):
            empty_b(t)
            fetch_n2(t)
        nc.vector.tensor_scalar(b_rows[last][:, 0:S], b_banks[last][:], size16[:, last : last + 1], None, ALU.mult)
        nc.vector.tensor_scalar(a_half[0][:, 0:S], a_banks[0][:], size_half[:, 0:1], None, ALU.mult)
        nc.vector.tensor_scalar(a_rows[0][:], a_half[0][:, 0:S], -2.0, None, ALU.mult)
        a_less_half(0)
        for t in range(1, last):
            empty_a(t)
            halve(t)
            smaller(t - 1)
            a_less_half(t)
        nc.scalar.activation(a_half[last][:, 0:S], a_banks[last][:], COPY, scale=size_half[:, last : last + 1])
        fetch_n2(last)
        a_n1 = sb("a_n1", [P, S], F32)
        nc.scalar.activation(a_n1[:], a_half[last][:].indirect(n1_l[:]), COPY)
        nc.vector.scalar_tensor_tensor(diff[last], a_banks[last][:], size16[:, last : last + 1], a_n1[:], ALU.mult, ALU.add)
        smaller(last - 1)
        for lo, hi in CHUNKS:
            nc.vector.tensor_tensor(low[:, last, lo:hi], h_wide[last][:, S + lo : S + hi], b_n2[last][:, lo:hi], ALU.min)

        z_grouped = [sb("z_grouped%d" % c, [P, widths[c], PACK], BF16) for c in range(2)]
        for c, (lo, hi) in enumerate(CHUNKS):
            for t in range(PACK):
                nc.scalar.activation(b_n3[c][:, t, :], b_rows[t][:].indirect(n3_l[:, lo // 16 : hi // 16]), COPY)
            nc.vector.tensor_tensor(
                z_grouped[c][:].rearrange("p (c i) t -> p c t i", i=2),
                low[:, :, lo:hi].rearrange("p t (c i) -> p c t i", i=2),
                b_n3[c][:].rearrange("p t (c i) -> p c t i", i=2),
                ALU.max,
            )
        z_codes = sb("z_codes", [P, S], U32)
        z_scale = sb("z_scale", [P, S], U8)
        for c, (lo, hi) in enumerate(CHUNKS):
            nc.vector.quantize_mx(
                out=z_codes[:, lo:hi].bitcast(FP8X4), scales=z_scale[:, lo:hi], in_=z_grouped[c][:].rearrange("p c t -> p (c t)")
            )
        first_banks = [psum.tile([P, HALF], F32, name="h_first%d" % half, tag="bank%d" % (PACK * half)) for half in range(2)]
        h_banks = {t: psum.tile([P, S], F32, name="h_bank%d" % t, tag="bank%d" % t) for t in range(1, PACK)}
        for t in range(PACK):
            for lo, hi in ((0, HALF), (HALF, widths[0]), CHUNKS[1]):
                nc.tensor.matmul_mx(
                    out=h_banks[t][:, lo:hi] if t else first_banks[lo // HALF][:, lo % HALF : lo % HALF + hi - lo],
                    lhsT=w_codes[:, t * P : (t + 1) * P].bitcast(FP8X4),
                    lhsT_scale=w_scale[:, t * P : (t + 1) * P],
                    rhs=z_codes[:, lo:hi].bitcast(FP8X4),
                    rhs_scale=z_scale[:, lo:hi],
                    start=True,
                    stop=True,
                )

        out_rows = out.rearrange("(p t) n -> p t n", t=PACK)
        pa = [sb("pa%d" % t, [P, S], F32) for t in range(PACK)]
        pb = [sb("pb%d" % t, [P, S], F32) for t in range(PACK)]
        upper = [sb("upper%d" % t, [P, S], F32) for t in range(PACK)]
        h_n4 = {t: sb("h_n4_%d" % t, [P, S], F32) for t in range(1, PACK)}
        h_n5 = {t: sb("h_n5_%d" % t, [P, S], F32) for t in range(1, PACK)}

        def clamp_above(t, lo, hi):
            nc.vector.scalar_tensor_tensor(upper[t][:, lo:hi], pb[t][:, lo:hi], 0.0, pa[t][:, lo:hi], ALU.max, ALU.min)

        def clamp_below(t, lo, hi):
            result = sb("result%d_%d" % (t, lo), [P, hi - lo], F32)
            nc.vector.scalar_tensor_tensor(result[:], pb[t][:, lo:hi], 0.0, upper[t][:, lo:hi], ALU.min, ALU.max)
            nc.sync.dma_start(out_rows[:, t, lo:hi], result[:])

        for half in range(2):
            nc.scalar.copy(h_wide[0][:, cols(half)], first_banks[half][:])
            nc.vector.tensor_scalar(neg_wide[:, cols(half)], first_banks[half][:], -1.0, None, ALU.mult)
        nc.vector.tensor_tensor(pa[0][:], neg_wide[:].indirect(n4_l[:]), h_rows[0], ALU.add)
        nc.vector.tensor_tensor(pb[0][:], h_wide[0][:].indirect(n5_l[:]), h_neg, ALU.add)
        for t in range(1, PACK):
            nc.scalar.copy(h_rows[t], h_banks[t][:])
            nc.scalar.activation(h_n4[t][:], h_wide[t][:].indirect(n4_l[:]), COPY)
            nc.scalar.activation(h_n5[t][:], h_wide[t][:].indirect(n5_l[:]), COPY)
            nc.vector.tensor_tensor(pa[t][:], h_rows[t], h_n4[t][:], ALU.subtract)
            clamp_above(t - 1, 0, S)
            nc.vector.tensor_tensor(pb[t][:], h_n5[t][:], h_rows[t], ALU.subtract)
            clamp_below(t - 1, 0, S)
        for half in range(2):
            clamp_above(last, half * HALF, (half + 1) * HALF)
        for half in range(2):
            clamp_below(last, half * HALF, (half + 1) * HALF)
